import numpy as np
import ml_dtypes

BF16 = ml_dtypes.bfloat16


def bf(x):
    return np.asarray(x, np.float32).astype(BF16)


def f32(x):
    return np.asarray(x, np.float32)


def f64(x):
    return np.asarray(x).astype(np.float64)


def striped(idx):
    return np.concatenate([l.reshape(-1, 16).T for l in idx])


def rows(idx, k):
    return np.tile(np.repeat(idx, 16, axis=0), (k // (16 * 8), 1))


def look(tab, idx):
    return np.take_along_axis(f64(tab), rows(idx, len(tab)), axis=1)


K, S, D, V, N, M = 128, 2048, 2, 1024, 2048, 256


def setup_inputs():
    return {"tab": f32(np.random.standard_normal((2, K, S))), "t": f32(0.5 * np.random.standard_normal((K, V))), "w": bf(np.random.standard_normal((K, M)) / np.sqrt(K)), "b": f32(0.5 * np.random.standard_normal((M, 1))), "offs": striped(np.stack([np.random.permutation(S)[:N] for _ in range(8)]))}


def reference(tab, t, w, b, offs):
    idx = np.stack([g.T.reshape(-1) for g in np.split(offs, 8)])
    a = [look(tab[1], idx[:, d * V:(d + 1) * V]) + f64(t) for d in range(D)]
    e = [np.exp(np.maximum(v, 0.2 * v)) for v in a]
    x = sum(e[d] * look(tab[0], idx[:, d * V:(d + 1) * V]) for d in range(D)) / sum(e)
    return np.maximum(f64(w).T @ x + f64(b), 0.0)

@@ -1,0 +1,70 @@
+import concourse.mybir as mybir
+
+BF16, F32, U16 = mybir.dt.bfloat16, mybir.dt.float32, mybir.dt.uint16
+ADD, SUB, MULT, MAX = mybir.AluOpType.add, mybir.AluOpType.subtract, mybir.AluOpType.mult, mybir.AluOpType.max
+SIGMOID, RELU = mybir.ActivationFunctionType.Sigmoid, mybir.ActivationFunctionType.Relu
+
+K, NODES, D, TARGETS, M = 128, 2048, 2, 1024, 256
+LANES = 16
+PIECE = 512
+SLOPE = 0.2
+M_BLOCKS = M // 128
+
+FLOPS = 2 * K * M * TARGETS
+
+
+def list_part(offsets, d, first, count):
+    start = (TARGETS * d + first) // LANES
+    return offsets[:, start : start + count // LANES]
+
+
+def tile_lookup_gat_relu_kernel(tc, tab, t, w, b, offs, out):
+    nc = tc.nc
+    with (
+        tc.tile_pool(name="held", bufs=1) as held,
+        tc.tile_pool(name="work", bufs=2) as work,
+        tc.psum_pool(name="psum", bufs=2) as psum,
+    ):
+        offsets = held.tile([K, D * TARGETS // LANES], U16, name="offsets")
+        scores = held.tile([K, NODES], F32, name="scores")
+        target = held.tile([K, TARGETS], F32, name="target")
+        values = held.tile([K, NODES], F32, name="values")
+        weights = held.tile([K, M], BF16, name="weights")
+        bias = held.tile([128, M_BLOCKS], F32, name="bias")
+
+        nc.sync.dma_start(offsets[:], offs)
+        nc.sync.dma_start(scores[:], tab[1])
+        nc.sync.dma_start(target[:], t)
+        nc.sync.dma_start(values[:], tab[0])
+        nc.sync.dma_start(weights[:], w)
+        with nc.allow_non_contiguous_dma(reason="256 bias values, one for each output row"):
+            nc.sync.dma_start(bias[:], b.rearrange("(c p) o -> p (c o)", p=128))
+
+        shares = []
+        for first in range(0, TARGETS, PIECE):
+            a = work.tile([K, D, PIECE], F32, name="a")
+            for d in range(D):
+                looked_up = scores[:].indirect(list_part(offsets, d, first, PIECE))
+                nc.vector.tensor_tensor(a[:, d, :], looked_up, target[:, first : first + PIECE], ADD)
+            leaky = work.tile([K, D, PIECE], F32, name="leaky")
+            nc.vector.scalar_tensor_tensor(leaky[:], a[:], SLOPE, a[:], MULT, MAX)
+            margin = work.tile([K, PIECE], F32, name="margin")
+            nc.vector.tensor_tensor(margin[:], leaky[:, 0, :], leaky[:, 1, :], SUB)
+            share = work.tile([K, D, PIECE], F32, name="share")
+            nc.scalar.activation(share[:, 0, :], margin[:], SIGMOID)
+            nc.scalar.activation(share[:, 1, :], margin[:], SIGMOID, scale=-1.0)
+            shares.append(share)
+
+        for first, share in zip(range(0, TARGETS, PIECE), shares):
+            weighted = work.tile([K, D, PIECE], F32, name="weighted")
+            for d in range(D):
+                looked_up = values[:].indirect(list_part(offsets, d, first, PIECE))
+                nc.vector.tensor_tensor(weighted[:, d, :], looked_up, share[:, d, :], MULT)
+            x = work.tile([K, PIECE], BF16, name="x")
+            nc.vector.tensor_tensor(x[:], weighted[:, 0, :], weighted[:, 1, :], ADD)
+            for c in range(M_BLOCKS):
+                dense = psum.tile([128, PIECE], F32, name="dense")
+                nc.tensor.matmul(dense[:], weights[:, 128 * c : 128 * (c + 1)], x[:], start=True, stop=True)
+                result = work.tile([128, PIECE], F32, name="result")
+                nc.scalar.activation(result[:], dense[:], RELU, bias=bias[:, c : c + 1])
+                nc.sync.dma_start(out[128 * c : 128 * (c + 1), first : first + PIECE], result[:])

@@ -23,7 +23,8 @@ def tile_lookup_gat_relu_kernel(tc, tab, t, w, b, offs, out):
     with (
         tc.tile_pool(name="held", bufs=1) as held,
         tc.tile_pool(name="work", bufs=2) as work,
-        tc.psum_pool(name="psum", bufs=2) as psum,
+        tc.tile_pool(name="results", bufs=6) as results,
+        tc.psum_pool(name="psum", bufs=6) as psum,
     ):
         offsets = held.tile([K, D * TARGETS // LANES], U16, name="offsets")
         scores = held.tile([K, NODES], F32, name="scores")
@@ -34,7 +35,8 @@ def tile_lookup_gat_relu_kernel(tc, tab, t, w, b, offs, out):
 
         nc.sync.dma_start(offsets[:], offs)
         nc.sync.dma_start(scores[:], tab[1])
-        nc.sync.dma_start(target[:], t)
+        for first in range(0, TARGETS, PIECE):
+            nc.sync.dma_start(target[:, first : first + PIECE], t[:, first : first + PIECE])
         nc.sync.dma_start(values[:], tab[0])
         nc.sync.dma_start(weights[:], w)
         with nc.allow_non_contiguous_dma(reason="256 bias values, one for each output row"):
@@ -55,16 +57,21 @@ def tile_lookup_gat_relu_kernel(tc, tab, t, w, b, offs, out):
             nc.scalar.activation(share[:, 1, :], margin[:], SIGMOID, scale=-1.0)
             shares.append(share)
 
-        for first, share in zip(range(0, TARGETS, PIECE), shares):
-            weighted = work.tile([K, D, PIECE], F32, name="weighted")
+        last = TARGETS - PIECE
+        for first, count in ((0, PIECE), (last, PIECE // 2), (last + PIECE // 2, PIECE // 2)):
+            share, at = shares[first // PIECE], first % PIECE
+            weighted = work.tile([K, D, count], F32, name="weighted")
             for d in range(D):
-                looked_up = values[:].indirect(list_part(offsets, d, first, PIECE))
-                nc.vector.tensor_tensor(weighted[:, d, :], looked_up, share[:, d, :], MULT)
-            x = work.tile([K, PIECE], BF16, name="x")
+                looked_up = values[:].indirect(list_part(offsets, d, first, count))
+                nc.vector.tensor_tensor(weighted[:, d, :], looked_up, share[:, d, at : at + count], MULT)
+            x = work.tile([K, count], BF16, name="x")
             nc.vector.tensor_tensor(x[:], weighted[:, 0, :], weighted[:, 1, :], ADD)
             for c in range(M_BLOCKS):
-                dense = psum.tile([128, PIECE], F32, name="dense")
+                dense = psum.tile([128, count], F32, name="dense")
                 nc.tensor.matmul(dense[:], weights[:, 128 * c : 128 * (c + 1)], x[:], start=True, stop=True)
-                result = work.tile([128, PIECE], F32, name="result")
-                nc.scalar.activation(result[:], dense[:], RELU, bias=bias[:, c : c + 1])
-                nc.sync.dma_start(out[128 * c : 128 * (c + 1), first : first + PIECE], result[:])
+                result = results.tile([128, count], F32, name="result")
+                if c == 1 and first + count == TARGETS:
+                    nc.vector.tensor_scalar(result[:], dense[:], bias[:, c : c + 1], 0.0, ADD, MAX)
+                else:
+                    nc.scalar.activation(result[:], dense[:], RELU, bias=bias[:, c : c + 1])
+                nc.sync.dma_start(out[128 * c : 128 * (c + 1), first : first + count], result[:])

import concourse.mybir as mybir

BF16, F32, U16 = mybir.dt.bfloat16, mybir.dt.float32, mybir.dt.uint16
ADD, SUB, MULT, MAX = mybir.AluOpType.add, mybir.AluOpType.subtract, mybir.AluOpType.mult, mybir.AluOpType.max
SIGMOID, RELU = mybir.ActivationFunctionType.Sigmoid, mybir.ActivationFunctionType.Relu

K, NODES, D, TARGETS, M = 128, 2048, 2, 1024, 256
LANES = 16
PIECE = 512
SLOPE = 0.2
M_BLOCKS = M // 128

FLOPS = 2 * K * M * TARGETS


def list_part(offsets, d, first, count):
    start = (TARGETS * d + first) // LANES
    return offsets[:, start : start + count // LANES]


def tile_lookup_gat_relu_kernel(tc, tab, t, w, b, offs, out):
    nc = tc.nc
    with (
        tc.tile_pool(name="held", bufs=1) as held,
        tc.tile_pool(name="work", bufs=2) as work,
        tc.tile_pool(name="results", bufs=6) as results,
        tc.psum_pool(name="psum", bufs=6) as psum,
    ):
        offsets = held.tile([K, D * TARGETS // LANES], U16, name="offsets")
        scores = held.tile([K, NODES], F32, name="scores")
        target = held.tile([K, TARGETS], F32, name="target")
        values = held.tile([K, NODES], F32, name="values")
        weights = held.tile([K, M], BF16, name="weights")
        bias = held.tile([128, M_BLOCKS], F32, name="bias")

        nc.sync.dma_start(offsets[:], offs)
        nc.sync.dma_start(scores[:], tab[1])
        for first in range(0, TARGETS, PIECE):
            nc.sync.dma_start(target[:, first : first + PIECE], t[:, first : first + PIECE])
        nc.sync.dma_start(values[:], tab[0])
        nc.sync.dma_start(weights[:], w)
        with nc.allow_non_contiguous_dma(reason="256 bias values, one for each output row"):
            nc.sync.dma_start(bias[:], b.rearrange("(c p) o -> p (c o)", p=128))

        shares = []
        for first in range(0, TARGETS, PIECE):
            a = work.tile([K, D, PIECE], F32, name="a")
            for d in range(D):
                looked_up = scores[:].indirect(list_part(offsets, d, first, PIECE))
                nc.vector.tensor_tensor(a[:, d, :], looked_up, target[:, first : first + PIECE], ADD)
            leaky = work.tile([K, D, PIECE], F32, name="leaky")
            nc.vector.scalar_tensor_tensor(leaky[:], a[:], SLOPE, a[:], MULT, MAX)
            margin = work.tile([K, PIECE], F32, name="margin")
            nc.vector.tensor_tensor(margin[:], leaky[:, 0, :], leaky[:, 1, :], SUB)
            share = work.tile([K, D, PIECE], F32, name="share")
            nc.scalar.activation(share[:, 0, :], margin[:], SIGMOID)
            nc.scalar.activation(share[:, 1, :], margin[:], SIGMOID, scale=-1.0)
            shares.append(share)

        last = TARGETS - PIECE
        for first, count in ((0, PIECE), (last, PIECE // 2), (last + PIECE // 2, PIECE // 2)):
            share, at = shares[first // PIECE], first % PIECE
            weighted = work.tile([K, D, count], F32, name="weighted")
            for d in range(D):
                looked_up = values[:].indirect(list_part(offsets, d, first, count))
                nc.vector.tensor_tensor(weighted[:, d, :], looked_up, share[:, d, at : at + count], MULT)
            x = work.tile([K, count], BF16, name="x")
            nc.vector.tensor_tensor(x[:], weighted[:, 0, :], weighted[:, 1, :], ADD)
            for c in range(M_BLOCKS):
                dense = psum.tile([128, count], F32, name="dense")
                nc.tensor.matmul(dense[:], weights[:, 128 * c : 128 * (c + 1)], x[:], start=True, stop=True)
                result = results.tile([128, count], F32, name="result")
                if c == 1 and first + count == TARGETS:
                    nc.vector.tensor_scalar(result[:], dense[:], bias[:, c : c + 1], 0.0, ADD, MAX)
                else:
                    nc.scalar.activation(result[:], dense[:], RELU, bias=bias[:, c : c + 1])
                nc.sync.dma_start(out[128 * c : 128 * (c + 1), first : first + count], result[:])
